import numpy as np
import ml_dtypes


def mxq(x, axis, fmt="e4m3"):
    dtype, down = {"e4m3": (ml_dtypes.float8_e4m3fn, 7), "e5m2": (ml_dtypes.float8_e5m2, 14)}[fmt]
    v = np.moveaxis(np.asarray(x, np.float32).astype(ml_dtypes.bfloat16).astype(np.float64), axis, -1)
    blocks = v.reshape(v.shape[:-1] + (-1, 32))
    amax = np.abs(blocks).max(-1, keepdims=True)
    byte = np.maximum(np.where(amax > 0, np.frexp(amax)[1] - 1 + 127, 0) - down, 1)
    scale = np.exp2(byte - 127.0)
    codes = (blocks / scale).astype(np.float32).astype(dtype).astype(np.float64)
    return np.moveaxis((codes * scale).reshape(v.shape), -1, axis)


WIDE = False


def mx_kscale(k):
    if not WIDE:
        return np.ones(k)
    levels = np.array([30, -30])
    if k % 512:
        return np.exp2(np.random.permutation(np.resize(levels, k // 32))).repeat(32)
    a = np.empty((k // 512, 16))
    for p in range(k // 512):
        a[p, :8] = np.random.permutation(np.resize(levels, 8))
        for g in range(8):
            far = levels[np.abs(levels - a[p, g]) >= 10]
            a[p, g + 8] = far[np.random.randint(len(far))]
    return np.exp2(a.ravel()).repeat(32)


def f64(x):
    return np.asarray(x).astype(np.float64)


T, D, H = 3072, 640, 512


def setup_inputs():
    n = np.random.standard_normal
    s1 = mx_kscale(T)[:, None]
    s2 = mx_kscale(T)[:, None]
    m = np.exp(0.5 * n((T, 1)))
    return {
        "x": (n((T, D)) * s1).astype(np.float32),
        "de": (m * n((T, H)) / np.sqrt(T) / s1).astype(np.float32),
        "dr": (m * n((T, D)) / np.sqrt(T) * s2).astype(np.float32),
        "e": (n((T, H)) / s2).astype(np.float32),
        "p": (0.1 * n((640, 512))).astype(np.float32),
    }


def reference(x, de, dr, e, p):
    x_ = mxq(f64(x), 0, "e4m3")
    de_ = mxq(f64(de), 0, "e5m2")
    dr_ = mxq(f64(dr), 0, "e5m2")
    e_ = mxq(f64(e), 0, "e4m3")
    y = x_.T @ de_ + dr_.T @ e_
    return f64(p) - 0.0625 * y

@@ -1,0 +1,144 @@
+from contextlib import ExitStack
+
+import concourse.mybir as mybir
+
+T, D, H = 3072, 640, 512
+LEARNING_RATE = 0.0625
+
+FLOPS = 4 * T * D * H
+
+F32 = mybir.dt.float32
+BF16 = mybir.dt.bfloat16
+U32 = mybir.dt.uint32
+U8 = mybir.dt.uint8
+E4M3 = mybir.dt.float8_e4m3fn_x4
+E5M2 = mybir.dt.float8_e5m2_x4
+MULT = mybir.AluOpType.mult
+ADD = mybir.AluOpType.add
+
+P = 128
+PACK = 4
+T_PASS = P * PACK
+PASSES = T // T_PASS
+D_TILE = 128
+D_TILES = D // D_TILE
+MAIN = 512
+
+
+def tile_mix_tied_sgd_kernel(tc, x, de, dr, e, p, out):
+    nc = tc.nc
+
+    with ExitStack() as ctx:
+        raw = ctx.enter_context(tc.tile_pool(name="raw", bufs=6))
+        grouped = ctx.enter_context(tc.tile_pool(name="grouped", bufs=3))
+        packed = ctx.enter_context(tc.tile_pool(name="packed", bufs=4))
+        keep = ctx.enter_context(tc.tile_pool(name="keep", bufs=1))
+        psum = ctx.enter_context(tc.psum_pool(name="psum", bufs=1))
+        ctx.enter_context(tc.manual_schedule())
+
+        acc = [psum.tile([P, H], F32, name=f"acc{b}") for b in range(D_TILES)]
+
+        def load(tag, source, k, cols):
+            width = cols.stop - cols.start
+            rows = keep.tile([P, PACK, width], F32, name=tag) if tag == "last" else raw.tile([P, PACK, width], F32, name=tag)
+            nc.sync.dma_start(
+                out=rows[:],
+                in_=source[k * T_PASS : (k + 1) * T_PASS, cols].rearrange("(q j) w -> q j w", j=PACK),
+            )
+            return rows
+
+        def interleave(copy, out, rows):
+            copy(out=out, in_=rows.rearrange("q j w -> q w j"))
+
+        def quantize(codes, scales, fmt, rows, cols):
+            nc.vector.quantize_mx(
+                out=codes[:, cols].bitcast(fmt),
+                scales=scales[:, cols],
+                in_=rows[:, cols, :].rearrange("q w j -> q (w j)"),
+            )
+
+        def multiply(b, wide, wide_fmt, narrow, narrow_fmt, start, stop):
+            cols = slice(b * D_TILE, (b + 1) * D_TILE)
+            nc.tensor.matmul_mx(
+                out=acc[b][:],
+                lhsT=wide[0][:, cols].bitcast(wide_fmt),
+                lhsT_scale=wide[1][:, cols],
+                rhs=narrow[0][:].bitcast(narrow_fmt),
+                rhs_scale=narrow[1][:],
+                start=start,
+                stop=stop,
+            )
+
+        def packed_pair(tag, width):
+            codes = packed.tile([P, width], U32, name=tag + "_codes", align_bytes=64)
+            scales = packed.tile([P, width], U8, name=tag + "_scales", align_bytes=64)
+            return codes, scales
+
+        def step(k, wide_src, wide_fmt, narrow_src, narrow_fmt, start):
+            n_raw = load("narrow_raw", narrow_src, k, slice(0, H))
+            w_raw = load("wide_raw", wide_src, k, slice(0, D))
+            n_grp = grouped.tile([P, H, PACK], BF16, name="narrow_grp", align_bytes=64)
+            w_grp = grouped.tile([P, D, PACK], BF16, name="wide_grp", align_bytes=64)
+            narrow = packed_pair("narrow", H)
+            wide = packed_pair("wide", D)
+            interleave(nc.scalar.copy, n_grp[:], n_raw[:])
+            interleave(nc.vector.tensor_copy, w_grp[:], w_raw[:])
+            quantize(narrow[0], narrow[1], narrow_fmt, n_grp, slice(0, H))
+            quantize(wide[0], wide[1], wide_fmt, w_grp, slice(0, MAIN))
+            quantize(wide[0], wide[1], wide_fmt, w_grp, slice(MAIN, D))
+            for b in range(D_TILES):
+                multiply(b, wide, wide_fmt, narrow, narrow_fmt, start, False)
+
+        for k in range(PASSES):
+            step(k, x, E4M3, de, E5M2, k == 0)
+            if k < PASSES - 1:
+                step(k, dr, E5M2, e, E4M3, False)
+
+        k = PASSES - 1
+        half = MAIN // 2
+        n_raw = load("narrow_raw", e, k, slice(0, H))
+        m_raw = load("narrow_raw", dr, k, slice(0, MAIN))
+        p_rows = p.rearrange("(b q) h -> q b h", q=P)
+        o_rows = out.rearrange("(b q) h -> q b h", q=P)
+        p01 = keep.tile([P, 2, H], F32, name="p01")
+        p23 = keep.tile([P, 2, H], F32, name="p23")
+        p4 = keep.tile([P, 1, H], F32, name="p4")
+        nc.sync.dma_start(out=p01[:], in_=p_rows[:, 0:2, :])
+        nc.sync.dma_start(out=p23[:], in_=p_rows[:, 2:4, :])
+        l_raw = load("last", dr, k, slice(MAIN, D))
+        nc.sync.dma_start(out=p4[:], in_=p_rows[:, 4:5, :])
+        p_tiles = [p01[:, 0, :], p01[:, 1, :], p23[:, 0, :], p23[:, 1, :], p4[:, 0, :]]
+
+        n_grp = grouped.tile([P, H, PACK], BF16, name="narrow_grp", align_bytes=64)
+        w_grp = grouped.tile([P, D, PACK], BF16, name="wide_grp", align_bytes=64)
+        narrow = packed_pair("narrow", H)
+        wide = packed_pair("wide", D)
+
+        def finish(b):
+            multiply(b, wide, E5M2, narrow, E4M3, False, True)
+
+        def update(b):
+            result = keep.tile([P, H], F32, name=f"result{b}")
+            nc.vector.scalar_tensor_tensor(
+                out=result[:], in0=acc[b][:], scalar=-LEARNING_RATE, in1=p_tiles[b], op0=MULT, op1=ADD
+            )
+            nc.sync.dma_start(out=o_rows[:, b, :], in_=result[:])
+
+        interleave(nc.scalar.copy, n_grp[:], n_raw[:])
+        quantize(narrow[0], narrow[1], E4M3, n_grp, slice(0, H))
+        interleave(nc.vector.tensor_copy, w_grp[:, 0:half, :], m_raw[:, :, 0:half])
+        interleave(nc.scalar.copy, w_grp[:, half:MAIN, :], m_raw[:, :, half:MAIN])
+        interleave(nc.scalar.copy, w_grp[:, MAIN:D, :], l_raw[:])
+        quantize(wide[0], wide[1], E5M2, w_grp, slice(0, half))
+        finish(0)
+        finish(1)
+        quantize(wide[0], wide[1], E5M2, w_grp, slice(half, MAIN))
+        finish(2)
+        finish(3)
+        update(0)
+        update(1)
+        update(2)
+        quantize(wide[0], wide[1], E5M2, w_grp, slice(MAIN, D))
+        finish(4)
+        update(3)
+        update(4)

@@ -22,6 +22,8 @@ T_PASS = P * PACK
 PASSES = T // T_PASS
 D_TILE = 128
 D_TILES = D // D_TILE
+SPLIT = 3 * D_TILE
+GROUPS = [(0, 3), (3, 2)]
 MAIN = 512
 
 
@@ -29,7 +31,7 @@ def tile_mix_tied_sgd_kernel(tc, x, de, dr, e, p, out):
     nc = tc.nc
 
     with ExitStack() as ctx:
-        raw = ctx.enter_context(tc.tile_pool(name="raw", bufs=6))
+        raw = ctx.enter_context(tc.tile_pool(name="raw", bufs=2))
         grouped = ctx.enter_context(tc.tile_pool(name="grouped", bufs=3))
         packed = ctx.enter_context(tc.tile_pool(name="packed", bufs=4))
         keep = ctx.enter_context(tc.tile_pool(name="keep", bufs=1))
@@ -38,107 +40,116 @@ def tile_mix_tied_sgd_kernel(tc, x, de, dr, e, p, out):
 
         acc = [psum.tile([P, H], F32, name=f"acc{b}") for b in range(D_TILES)]
 
-        def load(tag, source, k, cols):
-            width = cols.stop - cols.start
-            rows = keep.tile([P, PACK, width], F32, name=tag) if tag == "last" else raw.tile([P, PACK, width], F32, name=tag)
+        def load(pool, tag, source, first, count, cols):
+            rows = pool.tile([P, count, PACK, cols.stop - cols.start], F32, name=tag)
             nc.sync.dma_start(
                 out=rows[:],
-                in_=source[k * T_PASS : (k + 1) * T_PASS, cols].rearrange("(q j) w -> q j w", j=PACK),
+                in_=source[first * T_PASS : (first + count) * T_PASS, cols].rearrange(
+                    "(g q j) w -> q g j w", g=count, j=PACK
+                ),
             )
             return rows
 
-        def interleave(copy, out, rows):
-            copy(out=out, in_=rows.rearrange("q j w -> q w j"))
+        def interleave(copy, grp, grp_cols, rows):
+            copy(out=grp[:, grp_cols, :], in_=rows.rearrange("q j w -> q w j"))
 
-        def quantize(codes, scales, fmt, rows, cols):
+        def quantize(op, cols):
+            grp, codes, scales, fmt = op
             nc.vector.quantize_mx(
                 out=codes[:, cols].bitcast(fmt),
                 scales=scales[:, cols],
-                in_=rows[:, cols, :].rearrange("q w j -> q (w j)"),
+                in_=grp[:, cols, :].rearrange("q w j -> q (w j)"),
             )
 
-        def multiply(b, wide, wide_fmt, narrow, narrow_fmt, start, stop):
+        def multiply(b, wide, narrow, start, stop):
             cols = slice(b * D_TILE, (b + 1) * D_TILE)
             nc.tensor.matmul_mx(
                 out=acc[b][:],
-                lhsT=wide[0][:, cols].bitcast(wide_fmt),
-                lhsT_scale=wide[1][:, cols],
-                rhs=narrow[0][:].bitcast(narrow_fmt),
-                rhs_scale=narrow[1][:],
+                lhsT=wide[1][:, cols].bitcast(wide[3]),
+                lhsT_scale=wide[2][:, cols],
+                rhs=narrow[1][:].bitcast(narrow[3]),
+                rhs_scale=narrow[2][:],
                 start=start,
                 stop=stop,
             )
 
-        def packed_pair(tag, width):
+        def operand(tag, width, fmt):
+            grp = grouped.tile([P, width, PACK], BF16, name=tag + "_grp", align_bytes=64)
             codes = packed.tile([P, width], U32, name=tag + "_codes", align_bytes=64)
             scales = packed.tile([P, width], U8, name=tag + "_scales", align_bytes=64)
-            return codes, scales
+            return grp, codes, scales, fmt
 
-        def step(k, wide_src, wide_fmt, narrow_src, narrow_fmt, start):
-            n_raw = load("narrow_raw", narrow_src, k, slice(0, H))
-            w_raw = load("wide_raw", wide_src, k, slice(0, D))
-            n_grp = grouped.tile([P, H, PACK], BF16, name="narrow_grp", align_bytes=64)
-            w_grp = grouped.tile([P, D, PACK], BF16, name="wide_grp", align_bytes=64)
-            narrow = packed_pair("narrow", H)
-            wide = packed_pair("wide", D)
-            interleave(nc.scalar.copy, n_grp[:], n_raw[:])
-            interleave(nc.vector.tensor_copy, w_grp[:], w_raw[:])
-            quantize(narrow[0], narrow[1], narrow_fmt, n_grp, slice(0, H))
-            quantize(wide[0], wide[1], wide_fmt, w_grp, slice(0, MAIN))
-            quantize(wide[0], wide[1], wide_fmt, w_grp, slice(MAIN, D))
-            for b in range(D_TILES):
-                multiply(b, wide, wide_fmt, narrow, narrow_fmt, start, False)
-
-        for k in range(PASSES):
-            step(k, x, E4M3, de, E5M2, k == 0)
-            if k < PASSES - 1:
-                step(k, dr, E5M2, e, E4M3, False)
+        for first, count in GROUPS:
+            for wide_src, wide_fmt, narrow_src, narrow_fmt in ((x, E4M3, de, E5M2), (dr, E5M2, e, E4M3)):
+                n_raw = load(raw, "narrow_raw", narrow_src, first, count, slice(0, H))
+                w_raw = load(raw, "wide_raw", wide_src, first, count, slice(0, D))
+                for g in range(count):
+                    narrow = operand("narrow", H, narrow_fmt)
+                    wide = operand("wide", D, wide_fmt)
+                    interleave(nc.scalar.copy, narrow[0], slice(0, H), n_raw[:, g])
+                    interleave(nc.vector.tensor_copy, wide[0], slice(0, D), w_raw[:, g])
+                    quantize(narrow, slice(0, H))
+                    quantize(wide, slice(0, MAIN))
+                    quantize(wide, slice(MAIN, D))
+                    for b in range(D_TILES):
+                        multiply(b, wide, narrow, first + g == 0 and wide_src is x, False)
 
         k = PASSES - 1
-        half = MAIN // 2
-        n_raw = load("narrow_raw", e, k, slice(0, H))
-        m_raw = load("narrow_raw", dr, k, slice(0, MAIN))
+        x_raw = load(keep, "x_raw", x, k, 1, slice(0, D))
+        de_raw = load(keep, "de_raw", de, k, 1, slice(0, H))
+        e_raw = load(keep, "e_raw", e, k, 1, slice(0, H))
+        dra_raw = load(keep, "dra_raw", dr, k, 1, slice(0, SPLIT))
         p_rows = p.rearrange("(b q) h -> q b h", q=P)
         o_rows = out.rearrange("(b q) h -> q b h", q=P)
-        p01 = keep.tile([P, 2, H], F32, name="p01")
-        p23 = keep.tile([P, 2, H], F32, name="p23")
-        p4 = keep.tile([P, 1, H], F32, name="p4")
-        nc.sync.dma_start(out=p01[:], in_=p_rows[:, 0:2, :])
-        nc.sync.dma_start(out=p23[:], in_=p_rows[:, 2:4, :])
-        l_raw = load("last", dr, k, slice(MAIN, D))
-        nc.sync.dma_start(out=p4[:], in_=p_rows[:, 4:5, :])
-        p_tiles = [p01[:, 0, :], p01[:, 1, :], p23[:, 0, :], p23[:, 1, :], p4[:, 0, :]]
+        p_sb = keep.tile([P, D_TILES, H], F32, name="p_sb")
 
-        n_grp = grouped.tile([P, H, PACK], BF16, name="narrow_grp", align_bytes=64)
-        w_grp = grouped.tile([P, D, PACK], BF16, name="wide_grp", align_bytes=64)
-        narrow = packed_pair("narrow", H)
-        wide = packed_pair("wide", D)
+        def load_p(lo, hi):
+            nc.sync.dma_start(out=p_sb[:, lo:hi, :], in_=p_rows[:, lo:hi, :])
 
-        def finish(b):
-            multiply(b, wide, E5M2, narrow, E4M3, False, True)
+        load_p(0, 1)
+        drb_raw = load(keep, "drb_raw", dr, k, 1, slice(SPLIT, D))
+        load_p(1, 3)
+        load_p(3, 5)
+
+        x_op = operand("wide", D, E4M3)
+        de_op = operand("narrow", H, E5M2)
+        e_op = operand("narrow", H, E4M3)
+        dr_op = operand("wide", D, E5M2)
+        tiles = [slice(b * D_TILE, (b + 1) * D_TILE) for b in range(D_TILES)]
+        lower = slice(0, H // 2)
+        upper = slice(H // 2, H)
+
+        interleave(nc.vector.tensor_copy, x_op[0], slice(0, D), x_raw[:, 0])
+        interleave(nc.scalar.copy, de_op[0], upper, de_raw[:, 0, :, upper])
+        interleave(nc.vector.tensor_copy, de_op[0], lower, de_raw[:, 0, :, lower])
+        quantize(x_op, slice(0, MAIN))
+        quantize(x_op, slice(MAIN, D))
+        quantize(de_op, slice(0, H))
+        for b in range(D_TILES):
+            multiply(b, x_op, de_op, False, False)
 
         def update(b):
             result = keep.tile([P, H], F32, name=f"result{b}")
             nc.vector.scalar_tensor_tensor(
-                out=result[:], in0=acc[b][:], scalar=-LEARNING_RATE, in1=p_tiles[b], op0=MULT, op1=ADD
+                out=result[:], in0=acc[b][:], scalar=-LEARNING_RATE, in1=p_sb[:, b, :], op0=MULT, op1=ADD
             )
             nc.sync.dma_start(out=o_rows[:, b, :], in_=result[:])
 
-        interleave(nc.scalar.copy, n_grp[:], n_raw[:])
-        quantize(narrow[0], narrow[1], E4M3, n_grp, slice(0, H))
-        interleave(nc.vector.tensor_copy, w_grp[:, 0:half, :], m_raw[:, :, 0:half])
-        interleave(nc.scalar.copy, w_grp[:, half:MAIN, :], m_raw[:, :, half:MAIN])
-        interleave(nc.scalar.copy, w_grp[:, MAIN:D, :], l_raw[:])
-        quantize(wide[0], wide[1], E5M2, w_grp, slice(0, half))
-        finish(0)
-        finish(1)
-        quantize(wide[0], wide[1], E5M2, w_grp, slice(half, MAIN))
-        finish(2)
-        finish(3)
+        interleave(nc.vector.tensor_copy, e_op[0], lower, e_raw[:, 0, :, lower])
+        interleave(nc.scalar.copy, e_op[0], upper, e_raw[:, 0, :, upper])
+        quantize(e_op, slice(0, H))
+        interleave(nc.vector.tensor_copy, dr_op[0], tiles[0], dra_raw[:, 0, :, tiles[0]])
+        interleave(nc.scalar.copy, dr_op[0], tiles[1], dra_raw[:, 0, :, tiles[1]])
+        interleave(nc.vector.tensor_copy, dr_op[0], tiles[2], dra_raw[:, 0, :, tiles[2]])
+        interleave(nc.scalar.copy, dr_op[0], slice(SPLIT, D), drb_raw[:, 0])
+        for b in range(3):
+            quantize(dr_op, tiles[b])
+            multiply(b, dr_op, e_op, False, True)
         update(0)
         update(1)
+        quantize(dr_op, slice(SPLIT, D))
+        for b in (3, 4):
+            multiply(b, dr_op, e_op, False, True)
         update(2)
-        quantize(wide[0], wide[1], E5M2, w_grp, slice(MAIN, D))
-        finish(4)
         update(3)
         update(4)

@@ -22,8 +22,8 @@ T_PASS = P * PACK
 PASSES = T // T_PASS
 D_TILE = 128
 D_TILES = D // D_TILE
-SPLIT = 3 * D_TILE
-GROUPS = [(0, 3), (3, 2)]
+VECTOR_SHARE = 320
+GROUPS = [(0, 2), (2, 2), (4, 1)]
 MAIN = 512
 
 
@@ -31,7 +31,7 @@ def tile_mix_tied_sgd_kernel(tc, x, de, dr, e, p, out):
     nc = tc.nc
 
     with ExitStack() as ctx:
-        raw = ctx.enter_context(tc.tile_pool(name="raw", bufs=2))
+        raw = ctx.enter_context(tc.tile_pool(name="raw", bufs=3))
         grouped = ctx.enter_context(tc.tile_pool(name="grouped", bufs=3))
         packed = ctx.enter_context(tc.tile_pool(name="packed", bufs=4))
         keep = ctx.enter_context(tc.tile_pool(name="keep", bufs=1))
@@ -79,6 +79,12 @@ def tile_mix_tied_sgd_kernel(tc, x, de, dr, e, p, out):
             scales = packed.tile([P, width], U8, name=tag + "_scales", align_bytes=64)
             return grp, codes, scales, fmt
 
+        tiles = [slice(b * D_TILE, (b + 1) * D_TILE) for b in range(D_TILES)]
+        main = slice(0, MAIN)
+        rest = slice(MAIN, D)
+        lower = slice(0, VECTOR_SHARE)
+        upper = slice(VECTOR_SHARE, H)
+
         for first, count in GROUPS:
             for wide_src, wide_fmt, narrow_src, narrow_fmt in ((x, E4M3, de, E5M2), (dr, E5M2, e, E4M3)):
                 n_raw = load(raw, "narrow_raw", narrow_src, first, count, slice(0, H))
@@ -87,10 +93,11 @@ def tile_mix_tied_sgd_kernel(tc, x, de, dr, e, p, out):
                     narrow = operand("narrow", H, narrow_fmt)
                     wide = operand("wide", D, wide_fmt)
                     interleave(nc.scalar.copy, narrow[0], slice(0, H), n_raw[:, g])
-                    interleave(nc.vector.tensor_copy, wide[0], slice(0, D), w_raw[:, g])
+                    interleave(nc.scalar.copy, wide[0], rest, w_raw[:, g, :, rest])
+                    interleave(nc.vector.tensor_copy, wide[0], main, w_raw[:, g, :, main])
                     quantize(narrow, slice(0, H))
-                    quantize(wide, slice(0, MAIN))
-                    quantize(wide, slice(MAIN, D))
+                    quantize(wide, main)
+                    quantize(wide, rest)
                     for b in range(D_TILES):
                         multiply(b, wide, narrow, first + g == 0 and wide_src is x, False)
 
@@ -98,7 +105,7 @@ def tile_mix_tied_sgd_kernel(tc, x, de, dr, e, p, out):
         x_raw = load(keep, "x_raw", x, k, 1, slice(0, D))
         de_raw = load(keep, "de_raw", de, k, 1, slice(0, H))
         e_raw = load(keep, "e_raw", e, k, 1, slice(0, H))
-        dra_raw = load(keep, "dra_raw", dr, k, 1, slice(0, SPLIT))
+        dra_raw = load(keep, "dra_raw", dr, k, 1, main)
         p_rows = p.rearrange("(b q) h -> q b h", q=P)
         o_rows = out.rearrange("(b q) h -> q b h", q=P)
         p_sb = keep.tile([P, D_TILES, H], F32, name="p_sb")
@@ -106,24 +113,22 @@ def tile_mix_tied_sgd_kernel(tc, x, de, dr, e, p, out):
         def load_p(lo, hi):
             nc.sync.dma_start(out=p_sb[:, lo:hi, :], in_=p_rows[:, lo:hi, :])
 
-        load_p(0, 1)
-        drb_raw = load(keep, "drb_raw", dr, k, 1, slice(SPLIT, D))
-        load_p(1, 3)
-        load_p(3, 5)
+        load_p(0, 2)
+        drb_raw = load(keep, "drb_raw", dr, k, 1, rest)
+        load_p(2, 4)
+        load_p(4, 5)
 
         x_op = operand("wide", D, E4M3)
         de_op = operand("narrow", H, E5M2)
         e_op = operand("narrow", H, E4M3)
         dr_op = operand("wide", D, E5M2)
-        tiles = [slice(b * D_TILE, (b + 1) * D_TILE) for b in range(D_TILES)]
-        lower = slice(0, H // 2)
-        upper = slice(H // 2, H)
 
-        interleave(nc.vector.tensor_copy, x_op[0], slice(0, D), x_raw[:, 0])
+        interleave(nc.scalar.copy, x_op[0], rest, x_raw[:, 0, :, rest])
+        interleave(nc.vector.tensor_copy, x_op[0], main, x_raw[:, 0, :, main])
+        quantize(x_op, rest)
+        quantize(x_op, main)
         interleave(nc.scalar.copy, de_op[0], upper, de_raw[:, 0, :, upper])
         interleave(nc.vector.tensor_copy, de_op[0], lower, de_raw[:, 0, :, lower])
-        quantize(x_op, slice(0, MAIN))
-        quantize(x_op, slice(MAIN, D))
         quantize(de_op, slice(0, H))
         for b in range(D_TILES):
             multiply(b, x_op, de_op, False, False)
@@ -141,15 +146,15 @@ def tile_mix_tied_sgd_kernel(tc, x, de, dr, e, p, out):
         interleave(nc.vector.tensor_copy, dr_op[0], tiles[0], dra_raw[:, 0, :, tiles[0]])
         interleave(nc.scalar.copy, dr_op[0], tiles[1], dra_raw[:, 0, :, tiles[1]])
         interleave(nc.vector.tensor_copy, dr_op[0], tiles[2], dra_raw[:, 0, :, tiles[2]])
-        interleave(nc.scalar.copy, dr_op[0], slice(SPLIT, D), drb_raw[:, 0])
-        for b in range(3):
+        interleave(nc.scalar.copy, dr_op[0], tiles[3], dra_raw[:, 0, :, tiles[3]])
+        interleave(nc.scalar.copy, dr_op[0], rest, drb_raw[:, 0])
+        for b in range(4):
             quantize(dr_op, tiles[b])
             multiply(b, dr_op, e_op, False, True)
         update(0)
         update(1)
-        quantize(dr_op, slice(SPLIT, D))
-        for b in (3, 4):
-            multiply(b, dr_op, e_op, False, True)
+        quantize(dr_op, rest)
+        multiply(4, dr_op, e_op, False, True)
         update(2)
         update(3)
         update(4)

from contextlib import ExitStack

import concourse.mybir as mybir

T, D, H = 3072, 640, 512
LEARNING_RATE = 0.0625

FLOPS = 4 * T * D * H

F32 = mybir.dt.float32
BF16 = mybir.dt.bfloat16
U32 = mybir.dt.uint32
U8 = mybir.dt.uint8
E4M3 = mybir.dt.float8_e4m3fn_x4
E5M2 = mybir.dt.float8_e5m2_x4
MULT = mybir.AluOpType.mult
ADD = mybir.AluOpType.add

P = 128
PACK = 4
T_PASS = P * PACK
PASSES = T // T_PASS
D_TILE = 128
D_TILES = D // D_TILE
VECTOR_SHARE = 320
GROUPS = [(0, 2), (2, 2), (4, 1)]
MAIN = 512


def tile_mix_tied_sgd_kernel(tc, x, de, dr, e, p, out):
    nc = tc.nc

    with ExitStack() as ctx:
        raw = ctx.enter_context(tc.tile_pool(name="raw", bufs=3))
        grouped = ctx.enter_context(tc.tile_pool(name="grouped", bufs=3))
        packed = ctx.enter_context(tc.tile_pool(name="packed", bufs=4))
        keep = ctx.enter_context(tc.tile_pool(name="keep", bufs=1))
        psum = ctx.enter_context(tc.psum_pool(name="psum", bufs=1))
        ctx.enter_context(tc.manual_schedule())

        acc = [psum.tile([P, H], F32, name=f"acc{b}") for b in range(D_TILES)]

        def load(pool, tag, source, first, count, cols):
            rows = pool.tile([P, count, PACK, cols.stop - cols.start], F32, name=tag)
            nc.sync.dma_start(
                out=rows[:],
                in_=source[first * T_PASS : (first + count) * T_PASS, cols].rearrange(
                    "(g q j) w -> q g j w", g=count, j=PACK
                ),
            )
            return rows

        def interleave(copy, grp, grp_cols, rows):
            copy(out=grp[:, grp_cols, :], in_=rows.rearrange("q j w -> q w j"))

        def quantize(op, cols):
            grp, codes, scales, fmt = op
            nc.vector.quantize_mx(
                out=codes[:, cols].bitcast(fmt),
                scales=scales[:, cols],
                in_=grp[:, cols, :].rearrange("q w j -> q (w j)"),
            )

        def multiply(b, wide, narrow, start, stop):
            cols = slice(b * D_TILE, (b + 1) * D_TILE)
            nc.tensor.matmul_mx(
                out=acc[b][:],
                lhsT=wide[1][:, cols].bitcast(wide[3]),
                lhsT_scale=wide[2][:, cols],
                rhs=narrow[1][:].bitcast(narrow[3]),
                rhs_scale=narrow[2][:],
                start=start,
                stop=stop,
            )

        def operand(tag, width, fmt):
            grp = grouped.tile([P, width, PACK], BF16, name=tag + "_grp", align_bytes=64)
            codes = packed.tile([P, width], U32, name=tag + "_codes", align_bytes=64)
            scales = packed.tile([P, width], U8, name=tag + "_scales", align_bytes=64)
            return grp, codes, scales, fmt

        tiles = [slice(b * D_TILE, (b + 1) * D_TILE) for b in range(D_TILES)]
        main = slice(0, MAIN)
        rest = slice(MAIN, D)
        lower = slice(0, VECTOR_SHARE)
        upper = slice(VECTOR_SHARE, H)

        for first, count in GROUPS:
            for wide_src, wide_fmt, narrow_src, narrow_fmt in ((x, E4M3, de, E5M2), (dr, E5M2, e, E4M3)):
                n_raw = load(raw, "narrow_raw", narrow_src, first, count, slice(0, H))
                w_raw = load(raw, "wide_raw", wide_src, first, count, slice(0, D))
                for g in range(count):
                    narrow = operand("narrow", H, narrow_fmt)
                    wide = operand("wide", D, wide_fmt)
                    interleave(nc.scalar.copy, narrow[0], slice(0, H), n_raw[:, g])
                    interleave(nc.scalar.copy, wide[0], rest, w_raw[:, g, :, rest])
                    interleave(nc.vector.tensor_copy, wide[0], main, w_raw[:, g, :, main])
                    quantize(narrow, slice(0, H))
                    quantize(wide, main)
                    quantize(wide, rest)
                    for b in range(D_TILES):
                        multiply(b, wide, narrow, first + g == 0 and wide_src is x, False)

        k = PASSES - 1
        x_raw = load(keep, "x_raw", x, k, 1, slice(0, D))
        de_raw = load(keep, "de_raw", de, k, 1, slice(0, H))
        e_raw = load(keep, "e_raw", e, k, 1, slice(0, H))
        dra_raw = load(keep, "dra_raw", dr, k, 1, main)
        p_rows = p.rearrange("(b q) h -> q b h", q=P)
        o_rows = out.rearrange("(b q) h -> q b h", q=P)
        p_sb = keep.tile([P, D_TILES, H], F32, name="p_sb")

        def load_p(lo, hi):
            nc.sync.dma_start(out=p_sb[:, lo:hi, :], in_=p_rows[:, lo:hi, :])

        load_p(0, 2)
        drb_raw = load(keep, "drb_raw", dr, k, 1, rest)
        load_p(2, 4)
        load_p(4, 5)

        x_op = operand("wide", D, E4M3)
        de_op = operand("narrow", H, E5M2)
        e_op = operand("narrow", H, E4M3)
        dr_op = operand("wide", D, E5M2)

        interleave(nc.scalar.copy, x_op[0], rest, x_raw[:, 0, :, rest])
        interleave(nc.vector.tensor_copy, x_op[0], main, x_raw[:, 0, :, main])
        quantize(x_op, rest)
        quantize(x_op, main)
        interleave(nc.scalar.copy, de_op[0], upper, de_raw[:, 0, :, upper])
        interleave(nc.vector.tensor_copy, de_op[0], lower, de_raw[:, 0, :, lower])
        quantize(de_op, slice(0, H))
        for b in range(D_TILES):
            multiply(b, x_op, de_op, False, False)

        def update(b):
            result = keep.tile([P, H], F32, name=f"result{b}")
            nc.vector.scalar_tensor_tensor(
                out=result[:], in0=acc[b][:], scalar=-LEARNING_RATE, in1=p_sb[:, b, :], op0=MULT, op1=ADD
            )
            nc.sync.dma_start(out=o_rows[:, b, :], in_=result[:])

        interleave(nc.vector.tensor_copy, e_op[0], lower, e_raw[:, 0, :, lower])
        interleave(nc.scalar.copy, e_op[0], upper, e_raw[:, 0, :, upper])
        quantize(e_op, slice(0, H))
        interleave(nc.vector.tensor_copy, dr_op[0], tiles[0], dra_raw[:, 0, :, tiles[0]])
        interleave(nc.scalar.copy, dr_op[0], tiles[1], dra_raw[:, 0, :, tiles[1]])
        interleave(nc.vector.tensor_copy, dr_op[0], tiles[2], dra_raw[:, 0, :, tiles[2]])
        interleave(nc.scalar.copy, dr_op[0], tiles[3], dra_raw[:, 0, :, tiles[3]])
        interleave(nc.scalar.copy, dr_op[0], rest, drb_raw[:, 0])
        for b in range(4):
            quantize(dr_op, tiles[b])
            multiply(b, dr_op, e_op, False, True)
        update(0)
        update(1)
        quantize(dr_op, rest)
        multiply(4, dr_op, e_op, False, True)
        update(2)
        update(3)
        update(4)
